import numpy as np
import ml_dtypes


def mxq(x, axis, fmt="e4m3"):
    dtype, down = {"e4m3": (ml_dtypes.float8_e4m3fn, 7), "e5m2": (ml_dtypes.float8_e5m2, 14)}[fmt]
    v = np.moveaxis(np.asarray(x, np.float32).astype(ml_dtypes.bfloat16).astype(np.float64), axis, -1)
    blocks = v.reshape(v.shape[:-1] + (-1, 32))
    amax = np.abs(blocks).max(-1, keepdims=True)
    byte = np.maximum(np.where(amax > 0, np.frexp(amax)[1] - 1 + 127, 0) - down, 1)
    scale = np.exp2(byte - 127.0)
    codes = (blocks / scale).astype(np.float32).astype(dtype).astype(np.float64)
    return np.moveaxis((codes * scale).reshape(v.shape), -1, axis)


WIDE = False


def mx_kscale(k):
    if not WIDE:
        return np.ones(k)
    levels = np.array([10, -10, 5, -5, 0])
    if k % 512:
        return np.exp2(np.random.permutation(np.resize(levels, k // 32))).repeat(32)
    a = np.empty((k // 512, 16))
    for p in range(k // 512):
        a[p, :8] = np.random.permutation(np.resize(levels, 8))
        for g in range(8):
            far = levels[np.abs(levels - a[p, g]) >= 10]
            a[p, g + 8] = far[np.random.randint(len(far))]
    return np.exp2(a.ravel()).repeat(32)


def f64(x):
    return np.asarray(x).astype(np.float64)


def striped(idx):
    return np.tile(idx.reshape(-1, 16).T, (8, 1)).astype(np.uint16)


def unstriped(offs):
    return offs[:16].T.reshape(-1).astype(np.int64)


E2M1 = np.array([0.0, 0.5, 1.0, 1.5, 2.0, 3.0, 4.0, 6.0, -0.0, -0.5, -1.0, -1.5, -2.0, -3.0, -4.0, -6.0])


def pack_weight(w, fmt):
    k, n = w.shape
    w = f64(np.asarray(w, np.float32).astype(ml_dtypes.bfloat16)).reshape(k // 32, 32, n)
    amax = np.abs(w).max(1)
    if fmt == "e4m3":
        byte = np.frexp(amax)[1] - 1 + 127 - 7
    else:
        mant, ex = np.frexp(amax / 6.0)
        byte = np.where(mant > 0.5, ex, ex - 1) + 127
    byte = np.clip(np.where(amax > 0, byte, 1), 1, 254)
    scaled = (w * np.exp2(127.0 - byte)[:, None, :]).reshape(k, n).astype(np.float32)
    by_word = np.ascontiguousarray(scaled.reshape(k // 512, 128, 4, n).transpose(0, 1, 3, 2))
    if fmt == "e4m3":
        words = by_word.astype(ml_dtypes.float8_e4m3fn).view(np.uint8)
    else:
        c = by_word.astype(ml_dtypes.float4_e2m1fn).view(np.uint8) & 0xF
        words = (c[..., 0::2] | (c[..., 1::2] << 4)).reshape(k // 512, 128, 2 * n)
    return np.ascontiguousarray(words), np.ascontiguousarray(byte.astype(np.uint8).reshape(k // 512, 16, n))


def unpack_weight(words, scales, fmt):
    g, _, n = scales.shape
    words = np.ascontiguousarray(words).reshape(g, 128, n, -1)
    if fmt == "e4m3":
        vals = words.view(ml_dtypes.float8_e4m3fn).astype(np.float64)
    else:
        nib = np.empty((g, 128, n, 4), np.uint8)
        nib[..., 0::2] = words & 0xF
        nib[..., 1::2] = words >> 4
        vals = E2M1[nib]
    vals = vals * np.repeat(np.exp2(scales.astype(np.float64) - 127.0), 8, axis=1)[..., None]
    return vals.transpose(0, 1, 3, 2).reshape(g * 512, n)


K, T, E, C, N = 1024, 768, 24, 128, 256
TOP = 4


def by_expert(wq, xq):
    return np.concatenate([wq[e].T @ xq[:, e * C:(e + 1) * C] for e in range(E)], axis=1)


def setup_inputs():
    n = np.random.standard_normal
    s = mx_kscale(K)[:, None]
    deal = np.repeat(np.arange(E), C).reshape(TOP, T)[:, np.random.permutation(T)]
    deal = np.take_along_axis(deal, np.argsort(np.random.rand(TOP, T), axis=0), axis=0)
    for _ in range(8):
        s_, t_ = np.random.permutation(T).reshape(2, -1); r = np.random.randint(TOP, size=T // 2); x, y = deal[r, s_].copy(), deal[r, t_].copy()
        ok = ~((deal[:, s_] == y).any(0) | (deal[:, t_] == x).any(0)); deal[r[ok], s_[ok]] = y[ok]; deal[r[ok], t_[ok]] = x[ok]
    order = np.lexsort((np.random.rand(TOP * T), deal.reshape(-1)))
    slot_token = order % T; pos = np.empty(TOP * T, np.int64); pos[order] = np.arange(TOP * T); pos = pos.reshape(TOP, T)
    g = np.random.uniform(0.5, 1.5, (TOP, T)); g = g / g.sum(0)
    w = [pack_weight(m, "e2m1") for m in n((E, K, N)) / np.sqrt(K) / s[None]]
    return {
        "xT": (n((K, T)) * s).astype(np.float32),
        "w_words": np.stack([m[0] for m in w]),
        "w_scales": np.stack([m[1] for m in w]),
        "gate": np.stack([np.tile(r, (N, 1)) for r in g]).astype(np.float32),
        "offs": striped(slot_token),
        "pos1": striped(pos[0]),
        "pos2": striped(pos[1]),
        "pos3": striped(pos[2]),
        "pos4": striped(pos[3]),
    }


def reference(xT, w_words, w_scales, gate, offs, pos1, pos2, pos3, pos4):
    idx = unstriped(offs)
    w = np.stack([unpack_weight(w_words[e], w_scales[e], "e2m1") for e in range(E)])
    xq = mxq(f64(xT)[:, idx], 0, "e4m3")
    y = by_expert(w, xq)
    return sum(f64(gate[r]) * y[:, unstriped(p)] for r, p in enumerate((pos1, pos2, pos3, pos4)))

@@ -1,0 +1,192 @@
+from contextlib import ExitStack
+
+import concourse.mybir as mybir
+
+P = 128
+PACK = 4
+K, T, E, C, N = 1024, 768, 24, 128, 256
+TOP = 4
+PASSES = K // (P * PACK)
+HALVES = N // P
+SLOTS = E * C
+FLOPS = 2 * K * N * SLOTS
+
+F32 = mybir.dt.float32
+BF16 = mybir.dt.bfloat16
+I32 = mybir.dt.int32
+U32 = mybir.dt.uint32
+U16 = mybir.dt.uint16
+U8 = mybir.dt.uint8
+FP8X4 = mybir.dt.float8_e4m3fn_x4
+FP4X4 = mybir.dt.float4_e2m1fn_x4
+MULT = mybir.AluOpType.mult
+
+W_BYTES = 2 * N
+GROUP = 4
+CHUNK = GROUP * C
+CHUNKS = SLOTS // CHUNK
+LOADS = (((0, 384), (384, 640), (640, 768)), ((0, 256), (256, 512), (512, 768)))
+
+
+def tile_moe_tk_lin_none_kernel(
+    tc, xT, w_words, w_scales, gate, offs, pos1, pos2, pos3, pos4, out
+):
+    nc = tc.nc
+    with ExitStack() as ctx:
+        lists = ctx.enter_context(tc.tile_pool(name="lists", bufs=1))
+        keep = ctx.enter_context(tc.tile_pool(name="keep", bufs=1))
+        sums = ctx.enter_context(tc.tile_pool(name="sums", bufs=2))
+        psum = ctx.enter_context(tc.psum_pool(name="psum", bufs=6))
+
+        offs_t = lists.tile([P, SLOTS // 16], U16, name="offs_t")
+        pos_t = [lists.tile([P, T // 16], U16, name=f"pos{r}_t") for r in range(TOP)]
+
+        w_sc = keep.tile([P, E * PASSES, N], U8, name="w_sc", align_bytes=64)
+        tok_bytes = keep.tile([P, T], U8, name="tok_bytes", align_bytes=64)
+        slot_bytes = keep.tile([P, SLOTS], U8, name="slot_bytes", align_bytes=64)
+        slot_bytes1 = keep.tile([P, SLOTS], U8, name="slot_bytes1", align_bytes=64)
+        nc.gpsimd.memset(tok_bytes[:], 0)
+        nc.vector.memset(w_sc[:].rearrange("p a n -> p (a n)").bitcast(I32), 0)
+        nc.gpsimd.memset(slot_bytes1[:], 0)
+
+        x_view = xT.rearrange("(a p j) t -> a p j t", a=PASSES, p=P, j=PACK)
+        raw = {}
+        for a in range(PASSES):
+            for lo, hi in LOADS[a]:
+                tile = keep.tile([P, PACK, hi - lo], F32, name=f"raw{a}_{lo}")
+                nc.sync.dma_start(tile[:], x_view[a][:, :, lo:hi])
+                raw[a, lo] = tile
+            if a == 0:
+                nc.sync.dma_start(offs_t[:], offs)
+
+        s_view = w_scales.bitcast(I32).rearrange("e a q n -> q (e a) n")
+        for q in range(4):
+            nc.sync.dma_start(w_sc[32 * q : 32 * q + 4].bitcast(I32), s_view[4 * q : 4 * q + 4])
+        w_view = w_words.bitcast(I32).rearrange("e a p c -> p (e a) c")
+        w_t = []
+        for g in range(CHUNKS):
+            tile = keep.tile([P, GROUP * PASSES, W_BYTES], U8, name=f"w{g}", align_bytes=64)
+            nc.sync.dma_start(tile[:].bitcast(I32), w_view[:, g * GROUP * PASSES : (g + 1) * GROUP * PASSES])
+            w_t.append(tile)
+
+        grouped = [keep.tile([P, T, PACK], BF16, name=f"grouped{a}", align_bytes=64) for a in range(PASSES)]
+        codes = [keep.tile([P, T], U32, name=f"codes{a}", align_bytes=64) for a in range(PASSES)]
+        words = [keep.tile([P, SLOTS], U32, name=f"words{a}", align_bytes=64) for a in range(PASSES)]
+        y = [keep.tile([P, SLOTS], F32, name=f"y{h}") for h in range(HALVES)]
+        gate_t = [keep.tile([P, HALVES, T], F32, name=f"gate{r}") for r in range(TOP)]
+
+        def cast(engine_copy, a, load, lo, hi):
+            engine_copy(
+                grouped[a][:, lo:hi, :],
+                raw[a, load][:, :, lo - load : hi - load].rearrange("p j w -> p w j"),
+            )
+
+        def quantise(a, lo, hi):
+            nc.vector.quantize_mx(
+                out=codes[a][:, lo:hi].bitcast(FP8X4),
+                scales=tok_bytes[4 * a : P, lo:hi],
+                in_=grouped[a][:, lo:hi, :].rearrange("p w j -> p (w j)"),
+            )
+
+        def gather_words(a, lo, hi):
+            nc.vector.tensor_copy(words[a][:, lo:hi], codes[a][:].indirect(offs_t[:, lo // 16 : hi // 16]))
+
+        def gather_bytes(lo, hi):
+            nc.vector.tensor_copy(slot_bytes[:, lo:hi], tok_bytes[:].indirect(offs_t[:, lo // 16 : hi // 16]))
+
+        def experts(lo, hi):
+            for h in range(HALVES):
+                bank = psum.tile([P, CHUNK], F32, name="bank")
+                for e in range(lo // C, hi // C):
+                    cols = slice(e * C, (e + 1) * C)
+                    for a in range(PASSES):
+                        i = (e % GROUP) * PASSES + a
+                        nc.tensor.matmul_mx(
+                            out=bank[:, e * C - lo : (e + 1) * C - lo],
+                            lhsT=w_t[e // GROUP][:, i, 2 * P * h : 2 * P * (h + 1)].bitcast(FP4X4),
+                            lhsT_scale=w_sc[:, e * PASSES + a, P * h : P * (h + 1)],
+                            rhs=words[a][:, cols].bitcast(FP8X4),
+                            rhs_scale=(slot_bytes1 if a else slot_bytes)[:, cols],
+                            start=(a == 0),
+                            stop=(a == PASSES - 1),
+                        )
+                nc.scalar.copy(y[h][:, lo:hi], bank[:, 0 : hi - lo])
+
+        def gather_group(kind, g):
+            lo, hi = g * CHUNK, (g + 1) * CHUNK
+            if kind == "b":
+                gather_bytes(lo, hi)
+            else:
+                gather_words(kind, lo, hi)
+
+        def shift(lo, hi):
+            nc.scalar.dma_start(slot_bytes1[0:112, lo:hi].bitcast(I32), slot_bytes[4:116, lo:hi].bitcast(I32))
+
+        for (lo, hi), cut in zip(LOADS[0], (128, 480, 672)):
+            cast(nc.scalar.copy, 0, lo, lo, cut)
+            cast(nc.vector.tensor_copy, 0, lo, cut, hi)
+            if lo == 0:
+                quantise(0, 0, 256)
+                quantise(0, 256, 384)
+            else:
+                quantise(0, lo, hi)
+        for lo, hi in LOADS[1]:
+            cast(nc.scalar.copy, 1, lo, lo, hi)
+
+        gather_group(0, 0)
+        gather_group(0, 1)
+        gather_group(0, 2)
+        quantise(1, 0, 512)
+        gather_group(0, 3)
+        quantise(1, 512, 768)
+        for g in range(4):
+            gather_group("b", g)
+            if g % 2:
+                shift((g - 1) * CHUNK, (g + 1) * CHUNK)
+        for r, p in enumerate((pos1, pos2, pos3, pos4)):
+            nc.sync.dma_start(pos_t[r][:], p)
+        for r in range(TOP):
+            nc.sync.dma_start(gate_t[r][:], gate[r].rearrange("(h p) t -> p h t", p=P))
+        for g in range(CHUNKS - 1):
+            if g >= 4:
+                gather_group(0, g)
+            gather_group(1, g)
+            experts(g * CHUNK, (g + 1) * CHUNK)
+            if g < 2:
+                gather_group("b", 4 + g)
+            if g == 1:
+                shift(4 * CHUNK, 6 * CHUNK)
+        gather_group(0, CHUNKS - 1)
+        lo = (CHUNKS - 1) * CHUNK
+        for width in (256, 128, 128):
+            gather_words(1, lo, lo + width)
+            experts(lo, lo + width)
+            lo += width
+
+        def fetch(h, r, tile, lo, hi):
+            nc.vector.tensor_tensor(
+                tile[:, lo:hi], y[h][:].indirect(pos_t[r][:, lo // 16 : hi // 16]), gate_t[r][:, h, lo:hi], MULT
+            )
+
+        def finish(h, prod, part, lo, hi):
+            total = sums.tile([P, T], F32, name="total")
+            nc.vector.tensor_add(total[:, lo:hi], part[:, lo:hi], prod[:, lo:hi])
+            nc.sync.dma_start(out[h * P : (h + 1) * P, lo:hi], total[:, lo:hi])
+
+        left = None
+        for h in range(HALVES):
+            prod = [sums.tile([P, T], F32, name=f"prod{r}") for r in range(TOP)]
+            part = [sums.tile([P, T], F32, name=f"part{s}") for s in range(2)]
+            fetch(h, 0, prod[0], 0, T)
+            fetch(h, 1, prod[1], 0, T)
+            if left:
+                finish(*left)
+            fetch(h, 2, prod[2], 0, T)
+            nc.vector.tensor_add(part[0][:], prod[0][:], prod[1][:])
+            cut = T if h == 0 else 512
+            fetch(h, 3, prod[3], 0, cut)
+            nc.vector.tensor_add(part[1][:], part[0][:], prod[2][:])
+            left = (h, prod[3], part[1], 0, cut)
+        fetch(1, 3, prod[3], 512, T)
+        finish(*left)
+        finish(1, prod[3], part[1], 512, T)

@@ -25,7 +25,7 @@ W_BYTES = 2 * N
 GROUP = 4
 CHUNK = GROUP * C
 CHUNKS = SLOTS // CHUNK
-LOADS = (((0, 384), (384, 640), (640, 768)), ((0, 256), (256, 512), (512, 768)))
+LOADS = (((0, 512), (512, 768)), ((0, 512), (512, 768)))
 
 
 def tile_moe_tk_lin_none_kernel(
@@ -35,6 +35,7 @@ def tile_moe_tk_lin_none_kernel(
     with ExitStack() as ctx:
         lists = ctx.enter_context(tc.tile_pool(name="lists", bufs=1))
         keep = ctx.enter_context(tc.tile_pool(name="keep", bufs=1))
+        stream = ctx.enter_context(tc.tile_pool(name="stream", bufs=CHUNKS))
         sums = ctx.enter_context(tc.tile_pool(name="sums", bufs=2))
         psum = ctx.enter_context(tc.psum_pool(name="psum", bufs=6))
 
@@ -45,9 +46,9 @@ def tile_moe_tk_lin_none_kernel(
         tok_bytes = keep.tile([P, T], U8, name="tok_bytes", align_bytes=64)
         slot_bytes = keep.tile([P, SLOTS], U8, name="slot_bytes", align_bytes=64)
         slot_bytes1 = keep.tile([P, SLOTS], U8, name="slot_bytes1", align_bytes=64)
-        nc.gpsimd.memset(tok_bytes[:], 0)
+        nc.gpsimd.memset(tok_bytes[:].bitcast(I32), 0)
         nc.vector.memset(w_sc[:].rearrange("p a n -> p (a n)").bitcast(I32), 0)
-        nc.gpsimd.memset(slot_bytes1[:], 0)
+        nc.gpsimd.memset(slot_bytes1[:].bitcast(I32), 0)
 
         x_view = xT.rearrange("(a p j) t -> a p j t", a=PASSES, p=P, j=PACK)
         raw = {}
@@ -65,15 +66,17 @@ def tile_moe_tk_lin_none_kernel(
         w_view = w_words.bitcast(I32).rearrange("e a p c -> p (e a) c")
         w_t = []
         for g in range(CHUNKS):
-            tile = keep.tile([P, GROUP * PASSES, W_BYTES], U8, name=f"w{g}", align_bytes=64)
-            nc.sync.dma_start(tile[:].bitcast(I32), w_view[:, g * GROUP * PASSES : (g + 1) * GROUP * PASSES])
+            tile = stream.tile([P, GROUP * PASSES * W_BYTES], U8, name=f"w{g}", tag="stream", align_bytes=64)
+            tile = tile[:].rearrange("p (i c) -> p i c", c=W_BYTES)
+            nc.sync.dma_start(tile.bitcast(I32), w_view[:, g * GROUP * PASSES : (g + 1) * GROUP * PASSES])
             w_t.append(tile)
+        for r, p in enumerate((pos1, pos2, pos3, pos4)):
+            nc.sync.dma_start(pos_t[r][:], p)
 
         grouped = [keep.tile([P, T, PACK], BF16, name=f"grouped{a}", align_bytes=64) for a in range(PASSES)]
         codes = [keep.tile([P, T], U32, name=f"codes{a}", align_bytes=64) for a in range(PASSES)]
         words = [keep.tile([P, SLOTS], U32, name=f"words{a}", align_bytes=64) for a in range(PASSES)]
         y = [keep.tile([P, SLOTS], F32, name=f"y{h}") for h in range(HALVES)]
-        gate_t = [keep.tile([P, HALVES, T], F32, name=f"gate{r}") for r in range(TOP)]
 
         def cast(engine_copy, a, load, lo, hi):
             engine_copy(
@@ -120,16 +123,12 @@ def tile_moe_tk_lin_none_kernel(
                 gather_words(kind, lo, hi)
 
         def shift(lo, hi):
-            nc.scalar.dma_start(slot_bytes1[0:112, lo:hi].bitcast(I32), slot_bytes[4:116, lo:hi].bitcast(I32))
+            nc.sync.dma_start(slot_bytes1[0:112, lo:hi].bitcast(I32), slot_bytes[4:116, lo:hi].bitcast(I32))
 
-        for (lo, hi), cut in zip(LOADS[0], (128, 480, 672)):
+        for (lo, hi), cut in zip(LOADS[0], (160, 608)):
             cast(nc.scalar.copy, 0, lo, lo, cut)
             cast(nc.vector.tensor_copy, 0, lo, cut, hi)
-            if lo == 0:
-                quantise(0, 0, 256)
-                quantise(0, 256, 384)
-            else:
-                quantise(0, lo, hi)
+            quantise(0, lo, hi)
         for lo, hi in LOADS[1]:
             cast(nc.scalar.copy, 1, lo, lo, hi)
 
@@ -143,10 +142,7 @@ def tile_moe_tk_lin_none_kernel(
             gather_group("b", g)
             if g % 2:
                 shift((g - 1) * CHUNK, (g + 1) * CHUNK)
-        for r, p in enumerate((pos1, pos2, pos3, pos4)):
-            nc.sync.dma_start(pos_t[r][:], p)
-        for r in range(TOP):
-            nc.sync.dma_start(gate_t[r][:], gate[r].rearrange("(h p) t -> p h t", p=P))
+        gate_t = []
         for g in range(CHUNKS - 1):
             if g >= 4:
                 gather_group(0, g)
@@ -156,6 +152,11 @@ def tile_moe_tk_lin_none_kernel(
                 gather_group("b", 4 + g)
             if g == 1:
                 shift(4 * CHUNK, 6 * CHUNK)
+                for r in range(TOP):
+                    tile = stream.tile([P, HALVES * T], F32, name=f"gate{r}", tag="stream", align_bytes=64)
+                    tile = tile[:].rearrange("p (h t) -> p h t", h=HALVES)
+                    nc.sync.dma_start(tile, gate[r].rearrange("(h p) t -> p h t", p=P))
+                    gate_t.append(tile)
         gather_group(0, CHUNKS - 1)
         lo = (CHUNKS - 1) * CHUNK
         for width in (256, 128, 128):

@@ -60,6 +60,8 @@ def tile_moe_tk_lin_none_kernel(
             if a == 0:
                 nc.sync.dma_start(offs_t[:], offs)
 
+        for r, p in enumerate((pos1, pos2, pos3, pos4)):
+            nc.sync.dma_start(pos_t[r][:], p)
         s_view = w_scales.bitcast(I32).rearrange("e a q n -> q (e a) n")
         for q in range(4):
             nc.sync.dma_start(w_sc[32 * q : 32 * q + 4].bitcast(I32), s_view[4 * q : 4 * q + 4])
@@ -70,8 +72,6 @@ def tile_moe_tk_lin_none_kernel(
             tile = tile[:].rearrange("p (i c) -> p i c", c=W_BYTES)
             nc.sync.dma_start(tile.bitcast(I32), w_view[:, g * GROUP * PASSES : (g + 1) * GROUP * PASSES])
             w_t.append(tile)
-        for r, p in enumerate((pos1, pos2, pos3, pos4)):
-            nc.sync.dma_start(pos_t[r][:], p)
 
         grouped = [keep.tile([P, T, PACK], BF16, name=f"grouped{a}", align_bytes=64) for a in range(PASSES)]
         codes = [keep.tile([P, T], U32, name=f"codes{a}", align_bytes=64) for a in range(PASSES)]
@@ -123,7 +123,7 @@ def tile_moe_tk_lin_none_kernel(
                 gather_words(kind, lo, hi)
 
         def shift(lo, hi):
-            nc.sync.dma_start(slot_bytes1[0:112, lo:hi].bitcast(I32), slot_bytes[4:116, lo:hi].bitcast(I32))
+            nc.gpsimd.dma_start(slot_bytes1[0:112, lo:hi].bitcast(I32), slot_bytes[4:116, lo:hi].bitcast(I32))
 
         for (lo, hi), cut in zip(LOADS[0], (160, 608)):
             cast(nc.scalar.copy, 0, lo, lo, cut)
@@ -138,25 +138,21 @@ def tile_moe_tk_lin_none_kernel(
         quantise(1, 0, 512)
         gather_group(0, 3)
         quantise(1, 512, 768)
-        for g in range(4):
+        for g in range(CHUNKS):
             gather_group("b", g)
-            if g % 2:
-                shift((g - 1) * CHUNK, (g + 1) * CHUNK)
+            shift(g * CHUNK, (g + 1) * CHUNK)
+            if g >= 2:
+                gather_group(1, g - 2)
+                experts((g - 2) * CHUNK, (g - 1) * CHUNK)
         gate_t = []
-        for g in range(CHUNKS - 1):
-            if g >= 4:
-                gather_group(0, g)
-            gather_group(1, g)
-            experts(g * CHUNK, (g + 1) * CHUNK)
-            if g < 2:
-                gather_group("b", 4 + g)
-            if g == 1:
-                shift(4 * CHUNK, 6 * CHUNK)
-                for r in range(TOP):
-                    tile = stream.tile([P, HALVES * T], F32, name=f"gate{r}", tag="stream", align_bytes=64)
-                    tile = tile[:].rearrange("p (h t) -> p h t", h=HALVES)
-                    nc.sync.dma_start(tile, gate[r].rearrange("(h p) t -> p h t", p=P))
-                    gate_t.append(tile)
+        for r in range(TOP):
+            tile = stream.tile([P, HALVES * T], F32, name=f"gate{r}", tag="stream", align_bytes=64)
+            tile = tile[:].rearrange("p (h t) -> p h t", h=HALVES)
+            nc.sync.dma_start(tile, gate[r].rearrange("(h p) t -> p h t", p=P))
+            gate_t.append(tile)
+        gather_group(0, 4)
+        gather_group(1, 4)
+        experts(4 * CHUNK, 5 * CHUNK)
         gather_group(0, CHUNKS - 1)
         lo = (CHUNKS - 1) * CHUNK
         for width in (256, 128, 128):

@@ -36,6 +36,7 @@ def tile_moe_tk_lin_none_kernel(
         lists = ctx.enter_context(tc.tile_pool(name="lists", bufs=1))
         keep = ctx.enter_context(tc.tile_pool(name="keep", bufs=1))
         stream = ctx.enter_context(tc.tile_pool(name="stream", bufs=CHUNKS))
+        ring = ctx.enter_context(tc.tile_pool(name="ring", bufs=4))
         sums = ctx.enter_context(tc.tile_pool(name="sums", bufs=2))
         psum = ctx.enter_context(tc.psum_pool(name="psum", bufs=6))
 
@@ -60,8 +61,6 @@ def tile_moe_tk_lin_none_kernel(
             if a == 0:
                 nc.sync.dma_start(offs_t[:], offs)
 
-        for r, p in enumerate((pos1, pos2, pos3, pos4)):
-            nc.sync.dma_start(pos_t[r][:], p)
         s_view = w_scales.bitcast(I32).rearrange("e a q n -> q (e a) n")
         for q in range(4):
             nc.sync.dma_start(w_sc[32 * q : 32 * q + 4].bitcast(I32), s_view[4 * q : 4 * q + 4])
@@ -72,10 +71,12 @@ def tile_moe_tk_lin_none_kernel(
             tile = tile[:].rearrange("p (i c) -> p i c", c=W_BYTES)
             nc.sync.dma_start(tile.bitcast(I32), w_view[:, g * GROUP * PASSES : (g + 1) * GROUP * PASSES])
             w_t.append(tile)
+        for r, p in enumerate((pos1, pos2, pos3, pos4)):
+            nc.sync.dma_start(pos_t[r][:], p)
 
         grouped = [keep.tile([P, T, PACK], BF16, name=f"grouped{a}", align_bytes=64) for a in range(PASSES)]
         codes = [keep.tile([P, T], U32, name=f"codes{a}", align_bytes=64) for a in range(PASSES)]
-        words = [keep.tile([P, SLOTS], U32, name=f"words{a}", align_bytes=64) for a in range(PASSES)]
+        words = {}
         y = [keep.tile([P, SLOTS], F32, name=f"y{h}") for h in range(HALVES)]
 
         def cast(engine_copy, a, load, lo, hi):
@@ -92,7 +93,12 @@ def tile_moe_tk_lin_none_kernel(
             )
 
         def gather_words(a, lo, hi):
-            nc.vector.tensor_copy(words[a][:, lo:hi], codes[a][:].indirect(offs_t[:, lo // 16 : hi // 16]))
+            g = lo // CHUNK
+            if lo == g * CHUNK:
+                words[a, g] = ring.tile([P, CHUNK], U32, name=f"words{a}", align_bytes=64)
+            nc.vector.tensor_copy(
+                words[a, g][:, lo - g * CHUNK : hi - g * CHUNK], codes[a][:].indirect(offs_t[:, lo // 16 : hi // 16])
+            )
 
         def gather_bytes(lo, hi):
             nc.vector.tensor_copy(slot_bytes[:, lo:hi], tok_bytes[:].indirect(offs_t[:, lo // 16 : hi // 16]))
@@ -108,12 +114,15 @@ def tile_moe_tk_lin_none_kernel(
                             out=bank[:, e * C - lo : (e + 1) * C - lo],
                             lhsT=w_t[e // GROUP][:, i, 2 * P * h : 2 * P * (h + 1)].bitcast(FP4X4),
                             lhsT_scale=w_sc[:, e * PASSES + a, P * h : P * (h + 1)],
-                            rhs=words[a][:, cols].bitcast(FP8X4),
+                            rhs=words[a, e // GROUP][:, (e % GROUP) * C : (e % GROUP + 1) * C].bitcast(FP8X4),
                             rhs_scale=(slot_bytes1 if a else slot_bytes)[:, cols],
                             start=(a == 0),
                             stop=(a == PASSES - 1),
                         )
-                nc.scalar.copy(y[h][:, lo:hi], bank[:, 0 : hi - lo])
+                if h == 0 and hi == SLOTS:
+                    nc.vector.tensor_copy(y[h][:, lo:hi], bank[:, 0 : hi - lo])
+                else:
+                    nc.scalar.copy(y[h][:, lo:hi], bank[:, 0 : hi - lo])
 
         def gather_group(kind, g):
             lo, hi = g * CHUNK, (g + 1) * CHUNK

from contextlib import ExitStack

import concourse.mybir as mybir

P = 128
PACK = 4
K, T, E, C, N = 1024, 768, 24, 128, 256
TOP = 4
PASSES = K // (P * PACK)
HALVES = N // P
SLOTS = E * C
FLOPS = 2 * K * N * SLOTS

F32 = mybir.dt.float32
BF16 = mybir.dt.bfloat16
I32 = mybir.dt.int32
U32 = mybir.dt.uint32
U16 = mybir.dt.uint16
U8 = mybir.dt.uint8
FP8X4 = mybir.dt.float8_e4m3fn_x4
FP4X4 = mybir.dt.float4_e2m1fn_x4
MULT = mybir.AluOpType.mult

W_BYTES = 2 * N
GROUP = 4
CHUNK = GROUP * C
CHUNKS = SLOTS // CHUNK
LOADS = (((0, 512), (512, 768)), ((0, 512), (512, 768)))


def tile_moe_tk_lin_none_kernel(
    tc, xT, w_words, w_scales, gate, offs, pos1, pos2, pos3, pos4, out
):
    nc = tc.nc
    with ExitStack() as ctx:
        lists = ctx.enter_context(tc.tile_pool(name="lists", bufs=1))
        keep = ctx.enter_context(tc.tile_pool(name="keep", bufs=1))
        stream = ctx.enter_context(tc.tile_pool(name="stream", bufs=CHUNKS))
        ring = ctx.enter_context(tc.tile_pool(name="ring", bufs=4))
        sums = ctx.enter_context(tc.tile_pool(name="sums", bufs=2))
        psum = ctx.enter_context(tc.psum_pool(name="psum", bufs=6))

        offs_t = lists.tile([P, SLOTS // 16], U16, name="offs_t")
        pos_t = [lists.tile([P, T // 16], U16, name=f"pos{r}_t") for r in range(TOP)]

        w_sc = keep.tile([P, E * PASSES, N], U8, name="w_sc", align_bytes=64)
        tok_bytes = keep.tile([P, T], U8, name="tok_bytes", align_bytes=64)
        slot_bytes = keep.tile([P, SLOTS], U8, name="slot_bytes", align_bytes=64)
        slot_bytes1 = keep.tile([P, SLOTS], U8, name="slot_bytes1", align_bytes=64)
        nc.gpsimd.memset(tok_bytes[:].bitcast(I32), 0)
        nc.vector.memset(w_sc[:].rearrange("p a n -> p (a n)").bitcast(I32), 0)
        nc.gpsimd.memset(slot_bytes1[:].bitcast(I32), 0)

        x_view = xT.rearrange("(a p j) t -> a p j t", a=PASSES, p=P, j=PACK)
        raw = {}
        for a in range(PASSES):
            for lo, hi in LOADS[a]:
                tile = keep.tile([P, PACK, hi - lo], F32, name=f"raw{a}_{lo}")
                nc.sync.dma_start(tile[:], x_view[a][:, :, lo:hi])
                raw[a, lo] = tile
            if a == 0:
                nc.sync.dma_start(offs_t[:], offs)

        s_view = w_scales.bitcast(I32).rearrange("e a q n -> q (e a) n")
        for q in range(4):
            nc.sync.dma_start(w_sc[32 * q : 32 * q + 4].bitcast(I32), s_view[4 * q : 4 * q + 4])
        w_view = w_words.bitcast(I32).rearrange("e a p c -> p (e a) c")
        w_t = []
        for g in range(CHUNKS):
            tile = stream.tile([P, GROUP * PASSES * W_BYTES], U8, name=f"w{g}", tag="stream", align_bytes=64)
            tile = tile[:].rearrange("p (i c) -> p i c", c=W_BYTES)
            nc.sync.dma_start(tile.bitcast(I32), w_view[:, g * GROUP * PASSES : (g + 1) * GROUP * PASSES])
            w_t.append(tile)
        for r, p in enumerate((pos1, pos2, pos3, pos4)):
            nc.sync.dma_start(pos_t[r][:], p)

        grouped = [keep.tile([P, T, PACK], BF16, name=f"grouped{a}", align_bytes=64) for a in range(PASSES)]
        codes = [keep.tile([P, T], U32, name=f"codes{a}", align_bytes=64) for a in range(PASSES)]
        words = {}
        y = [keep.tile([P, SLOTS], F32, name=f"y{h}") for h in range(HALVES)]

        def cast(engine_copy, a, load, lo, hi):
            engine_copy(
                grouped[a][:, lo:hi, :],
                raw[a, load][:, :, lo - load : hi - load].rearrange("p j w -> p w j"),
            )

        def quantise(a, lo, hi):
            nc.vector.quantize_mx(
                out=codes[a][:, lo:hi].bitcast(FP8X4),
                scales=tok_bytes[4 * a : P, lo:hi],
                in_=grouped[a][:, lo:hi, :].rearrange("p w j -> p (w j)"),
            )

        def gather_words(a, lo, hi):
            g = lo // CHUNK
            if lo == g * CHUNK:
                words[a, g] = ring.tile([P, CHUNK], U32, name=f"words{a}", align_bytes=64)
            nc.vector.tensor_copy(
                words[a, g][:, lo - g * CHUNK : hi - g * CHUNK], codes[a][:].indirect(offs_t[:, lo // 16 : hi // 16])
            )

        def gather_bytes(lo, hi):
            nc.vector.tensor_copy(slot_bytes[:, lo:hi], tok_bytes[:].indirect(offs_t[:, lo // 16 : hi // 16]))

        def experts(lo, hi):
            for h in range(HALVES):
                bank = psum.tile([P, CHUNK], F32, name="bank")
                for e in range(lo // C, hi // C):
                    cols = slice(e * C, (e + 1) * C)
                    for a in range(PASSES):
                        i = (e % GROUP) * PASSES + a
                        nc.tensor.matmul_mx(
                            out=bank[:, e * C - lo : (e + 1) * C - lo],
                            lhsT=w_t[e // GROUP][:, i, 2 * P * h : 2 * P * (h + 1)].bitcast(FP4X4),
                            lhsT_scale=w_sc[:, e * PASSES + a, P * h : P * (h + 1)],
                            rhs=words[a, e // GROUP][:, (e % GROUP) * C : (e % GROUP + 1) * C].bitcast(FP8X4),
                            rhs_scale=(slot_bytes1 if a else slot_bytes)[:, cols],
                            start=(a == 0),
                            stop=(a == PASSES - 1),
                        )
                if h == 0 and hi == SLOTS:
                    nc.vector.tensor_copy(y[h][:, lo:hi], bank[:, 0 : hi - lo])
                else:
                    nc.scalar.copy(y[h][:, lo:hi], bank[:, 0 : hi - lo])

        def gather_group(kind, g):
            lo, hi = g * CHUNK, (g + 1) * CHUNK
            if kind == "b":
                gather_bytes(lo, hi)
            else:
                gather_words(kind, lo, hi)

        def shift(lo, hi):
            nc.gpsimd.dma_start(slot_bytes1[0:112, lo:hi].bitcast(I32), slot_bytes[4:116, lo:hi].bitcast(I32))

        for (lo, hi), cut in zip(LOADS[0], (160, 608)):
            cast(nc.scalar.copy, 0, lo, lo, cut)
            cast(nc.vector.tensor_copy, 0, lo, cut, hi)
            quantise(0, lo, hi)
        for lo, hi in LOADS[1]:
            cast(nc.scalar.copy, 1, lo, lo, hi)

        gather_group(0, 0)
        gather_group(0, 1)
        gather_group(0, 2)
        quantise(1, 0, 512)
        gather_group(0, 3)
        quantise(1, 512, 768)
        for g in range(CHUNKS):
            gather_group("b", g)
            shift(g * CHUNK, (g + 1) * CHUNK)
            if g >= 2:
                gather_group(1, g - 2)
                experts((g - 2) * CHUNK, (g - 1) * CHUNK)
        gate_t = []
        for r in range(TOP):
            tile = stream.tile([P, HALVES * T], F32, name=f"gate{r}", tag="stream", align_bytes=64)
            tile = tile[:].rearrange("p (h t) -> p h t", h=HALVES)
            nc.sync.dma_start(tile, gate[r].rearrange("(h p) t -> p h t", p=P))
            gate_t.append(tile)
        gather_group(0, 4)
        gather_group(1, 4)
        experts(4 * CHUNK, 5 * CHUNK)
        gather_group(0, CHUNKS - 1)
        lo = (CHUNKS - 1) * CHUNK
        for width in (256, 128, 128):
            gather_words(1, lo, lo + width)
            experts(lo, lo + width)
            lo += width

        def fetch(h, r, tile, lo, hi):
            nc.vector.tensor_tensor(
                tile[:, lo:hi], y[h][:].indirect(pos_t[r][:, lo // 16 : hi // 16]), gate_t[r][:, h, lo:hi], MULT
            )

        def finish(h, prod, part, lo, hi):
            total = sums.tile([P, T], F32, name="total")
            nc.vector.tensor_add(total[:, lo:hi], part[:, lo:hi], prod[:, lo:hi])
            nc.sync.dma_start(out[h * P : (h + 1) * P, lo:hi], total[:, lo:hi])

        left = None
        for h in range(HALVES):
            prod = [sums.tile([P, T], F32, name=f"prod{r}") for r in range(TOP)]
            part = [sums.tile([P, T], F32, name=f"part{s}") for s in range(2)]
            fetch(h, 0, prod[0], 0, T)
            fetch(h, 1, prod[1], 0, T)
            if left:
                finish(*left)
            fetch(h, 2, prod[2], 0, T)
            nc.vector.tensor_add(part[0][:], prod[0][:], prod[1][:])
            cut = T if h == 0 else 512
            fetch(h, 3, prod[3], 0, cut)
            nc.vector.tensor_add(part[1][:], part[0][:], prod[2][:])
            left = (h, prod[3], part[1], 0, cut)
        fetch(1, 3, prod[3], 512, T)
        finish(*left)
        finish(1, prod[3], part[1], 512, T)
